import numpy as np
import ml_dtypes


def mxq(x, axis, fmt="e4m3"):
    dtype, down = {"e4m3": (ml_dtypes.float8_e4m3fn, 7), "e5m2": (ml_dtypes.float8_e5m2, 14)}[fmt]
    v = np.moveaxis(np.asarray(x, np.float32).astype(ml_dtypes.bfloat16).astype(np.float64), axis, -1)
    blocks = v.reshape(v.shape[:-1] + (-1, 32))
    amax = np.abs(blocks).max(-1, keepdims=True)
    byte = np.maximum(np.where(amax > 0, np.frexp(amax)[1] - 1 + 127, 0) - down, 1)
    scale = np.exp2(byte - 127.0)
    codes = (blocks / scale).astype(np.float32).astype(dtype).astype(np.float64)
    return np.moveaxis((codes * scale).reshape(v.shape), -1, axis)


WIDE = False


def mx_kscale(k):
    if not WIDE:
        return np.ones(k)
    levels = np.array([10, -10, 5, -5, 0])
    if k % 512:
        return np.exp2(np.random.permutation(np.resize(levels, k // 32))).repeat(32)
    a = np.empty((k // 512, 16))
    for p in range(k // 512):
        a[p, :8] = np.random.permutation(np.resize(levels, 8))
        for g in range(8):
            far = levels[np.abs(levels - a[p, g]) >= 10]
            a[p, g + 8] = far[np.random.randint(len(far))]
    return np.exp2(a.ravel()).repeat(32)


def f64(x):
    return np.asarray(x).astype(np.float64)


def striped8(idx):
    return np.concatenate([v.reshape(-1, 16).T for v in idx]).astype(np.uint16)


def unstriped8(offs):
    return np.stack([offs[16 * g:16 * g + 16].T.reshape(-1) for g in range(8)]).astype(np.int64)


E2M1 = np.array([0.0, 0.5, 1.0, 1.5, 2.0, 3.0, 4.0, 6.0, -0.0, -0.5, -1.0, -1.5, -2.0, -3.0, -4.0, -6.0])


def pack_weight(w, fmt):
    k, n = w.shape
    w = f64(np.asarray(w, np.float32).astype(ml_dtypes.bfloat16)).reshape(k // 32, 32, n)
    amax = np.abs(w).max(1)
    if fmt == "e4m3":
        byte = np.frexp(amax)[1] - 1 + 127 - 7
    else:
        mant, ex = np.frexp(amax / 6.0)
        byte = np.where(mant > 0.5, ex, ex - 1) + 127
    byte = np.clip(np.where(amax > 0, byte, 1), 1, 254)
    scaled = (w * np.exp2(127.0 - byte)[:, None, :]).reshape(k, n).astype(np.float32)
    by_word = np.ascontiguousarray(scaled.reshape(k // 512, 128, 4, n).transpose(0, 1, 3, 2))
    if fmt == "e4m3":
        words = by_word.astype(ml_dtypes.float8_e4m3fn).view(np.uint8)
    else:
        c = by_word.astype(ml_dtypes.float4_e2m1fn).view(np.uint8) & 0xF
        words = (c[..., 0::2] | (c[..., 1::2] << 4)).reshape(k // 512, 128, 2 * n)
    return np.ascontiguousarray(words), np.ascontiguousarray(byte.astype(np.uint8).reshape(k // 512, 16, n))


def unpack_weight(words, scales, fmt):
    g, _, n = scales.shape
    words = np.ascontiguousarray(words).reshape(g, 128, n, -1)
    if fmt == "e4m3":
        vals = words.view(ml_dtypes.float8_e4m3fn).astype(np.float64)
    else:
        nib = np.empty((g, 128, n, 4), np.uint8)
        nib[..., 0::2] = words & 0xF
        nib[..., 1::2] = words >> 4
        vals = E2M1[nib]
    vals = vals * np.repeat(np.exp2(scales.astype(np.float64) - 127.0), 8, axis=1)[..., None]
    return vals.transpose(0, 1, 3, 2).reshape(g * 512, n)


K, M, T, S = 1536, 1024, 1024, 512


def setup_inputs():
    n = np.random.standard_normal
    s = mx_kscale(K)[:, None]
    u = mx_kscale(512)[:, None]
    p_w4 = pack_weight(n((K, M)) / np.sqrt(K) / s, "e2m1")
    return {
        "xT": (n((K, T)) * s).astype(np.float32),
        "w4_words": p_w4[0],
        "w4_scales": p_w4[1],
        "down": (n((K, 512)) / np.sqrt(K) / s * u.T).astype(np.float32),
        "up": (0.5 * n((512, M)) / np.sqrt(512) / u).astype(np.float32),
        "wgt": np.repeat(np.random.uniform(0.5, 2.0, (8, S)), 16, axis=0).astype(np.float32),
        "b": (0.3 * n(1024)).astype(np.float32),
        "wgo": np.repeat(np.random.uniform(0.5, 2.0, (8, S)), 16, axis=0).astype(np.float32),
        "offs": striped8(np.stack([np.random.permutation(T)[:S] for _ in range(8)])),
        "offs2": striped8(np.stack([np.random.permutation(T)[:S] for _ in range(8)])),
    }


def reference(xT, w4_words, w4_scales, down, up, wgt, b, wgo, offs, offs2):
    idx = unstriped8(offs)
    group = np.arange(K) % 512 // 64
    xg = f64(wgt)[np.arange(K) // 4 % 128] * f64(xT)[np.arange(K)[:, None], idx[group]]
    xT_ = mxq(xg, 0, "e4m3")
    w4_ = unpack_weight(w4_words, w4_scales, "e2m1")
    down_ = mxq(f64(down), 0, "e4m3")
    up_ = mxq(f64(up), 0, "e4m3")
    h_ = mxq(down_.T @ xT_, 0, "e4m3")
    y = w4_.T @ xT_ + up_.T @ h_
    place = unstriped8(offs2)[np.arange(M) % 128 // 16]
    out = np.zeros((M, T))
    out[np.arange(M)[:, None], place] = f64(wgo)[np.arange(M) % 128] * (y + f64(b)[:, None])
    return out

@@ -1,0 +1,237 @@
+from contextlib import ExitStack
+
+import concourse.mybir as mybir
+from concourse.masks import make_identity
+
+K, M, T, S, R = 1536, 1024, 1024, 512, 512
+FLOPS = 2 * S * (K * R + K * M + R * M)
+
+F32 = mybir.dt.float32
+BF16 = mybir.dt.bfloat16
+I32 = mybir.dt.int32
+U32 = mybir.dt.uint32
+U16 = mybir.dt.uint16
+U8 = mybir.dt.uint8
+FP8X4 = mybir.dt.float8_e4m3fn_x4
+FP4X4 = mybir.dt.float4_e2m1fn_x4
+MULT = mybir.AluOpType.mult
+IDENTITY = mybir.ActivationFunctionType.Identity
+
+P = 128
+PACK = 4
+K_PASS = P * PACK
+PASSES = K // K_PASS
+HALF = S // 2
+QUARTER = S // 4
+TILES = M // P
+UP_CHUNK = 256
+EARLY = 2
+PAGES = 3
+DOWN_SPLIT = 40
+
+
+def tile_list_hboth_l_bias_kernel(tc, xT, w4_words, w4_scales, down, up, wgt, b, wgo, offs, offs2, out):
+    nc = tc.nc
+    with ExitStack() as ctx:
+        keep = ctx.enter_context(tc.tile_pool(name="keep", bufs=1))
+        ring = ctx.enter_context(tc.tile_pool(name="ring", bufs=3))
+        h_psum = ctx.enter_context(tc.psum_pool(name="h_psum", bufs=1))
+        y_psum = ctx.enter_context(tc.psum_pool(name="y_psum", bufs=4))
+
+        def held(name, shape, dtype):
+            return keep.tile(shape, dtype, name=name, align_bytes=64)
+
+        picks = keep.tile([P, S // 16], U16, name="picks")
+        places = keep.tile([P, S // 16], U16, name="places")
+        wgt_sb = held("wgt_sb", [P, S], F32)
+        wgo_sb = held("wgo_sb", [P, S], F32)
+        x_planes = [[held("x_%d_%d" % (a, i), [P, T], F32) for i in range(PACK)] for a in range(PASSES)]
+        down_raw = [held("down_raw%d" % a, [P, PACK, R], F32) for a in range(PASSES)]
+        up_raw = [held("up_raw%d" % u, [P, PACK, UP_CHUNK], F32) for u in range(M // UP_CHUNK)]
+        early_cols = EARLY * P
+        w4_early = held("w4_early", [P, PASSES, 2 * early_cols], U8)
+        w4_late = held("w4_late", [P, PASSES, 2 * (M - early_cols)], U8)
+        w4_plane = held("w4_plane", [P, PASSES, M], U8)
+        b_rows = held("b_rows", [P, P], F32)
+        ident = held("ident", [P, P], F32)
+        b_cols = held("b_cols", [P, TILES], F32)
+        pages = [held("page%d" % n, [P, T], F32) for n in range(PAGES)]
+
+        x_rows = xT.rearrange("(a p i) t -> a i p t", p=P, i=PACK)
+        down_rows = down.rearrange("(a p i) r -> a p i r", p=P, i=PACK)
+        up_rows = up.rearrange("(p i) n -> p i n", i=PACK)
+        w4_rows = w4_words.rearrange("a p n -> p a n")
+
+        make_identity(nc, ident[:])
+        nc.gpsimd.memset(b_rows[:], 0.0)
+        nc.gpsimd.dma_start(out=b_rows[0:TILES, :], in_=b.rearrange("(c p) -> c p", p=P))
+        nc.vector.memset(w4_plane[:].rearrange("p a n -> p (a n)").bitcast(I32), 0)
+        for q in range(4):
+            nc.gpsimd.dma_start(
+                out=w4_plane[32 * q : 32 * q + 4, :, :].bitcast(I32),
+                in_=w4_scales[:, 4 * q : 4 * q + 4, :].rearrange("a r n -> r a n").bitcast(I32),
+            )
+        for page in pages:
+            nc.vector.memset(page[:], 0.0)
+
+        nc.sync.dma_start(picks[:], offs)
+        nc.sync.dma_start(out=x_planes[0][0][:], in_=x_rows[0, 0])
+        nc.sync.dma_start(out=wgt_sb[:], in_=wgt)
+        for i in range(1, PACK):
+            nc.sync.dma_start(out=x_planes[0][i][:], in_=x_rows[0, i])
+        nc.sync.dma_start(out=down_raw[0][:], in_=down_rows[0])
+        for i in range(PACK):
+            nc.sync.dma_start(out=x_planes[1][i][:], in_=x_rows[1, i])
+        nc.sync.dma_start(out=down_raw[1][:], in_=down_rows[1])
+        for i in range(PACK):
+            nc.sync.dma_start(out=x_planes[2][i][:], in_=x_rows[2, i])
+        nc.sync.dma_start(out=down_raw[2][:], in_=down_rows[2])
+        nc.sync.dma_start(out=up_raw[0][:], in_=up_rows[:, :, 0:UP_CHUNK])
+        nc.sync.dma_start(out=w4_early[:].bitcast(I32), in_=w4_rows[:, :, 0 : 2 * early_cols].bitcast(I32))
+        nc.sync.dma_start(out=wgo_sb[:], in_=wgo)
+        nc.sync.dma_start(places[:], offs2)
+        nc.sync.dma_start(out=up_raw[1][:], in_=up_rows[:, :, UP_CHUNK : 2 * UP_CHUNK])
+        nc.sync.dma_start(out=w4_late[:].bitcast(I32), in_=w4_rows[:, :, 2 * early_cols :].bitcast(I32))
+        for u in range(2, M // UP_CHUNK):
+            nc.sync.dma_start(out=up_raw[u][:], in_=up_rows[:, :, u * UP_CHUNK : (u + 1) * UP_CHUNK])
+
+        b_bank = y_psum.tile([P, P], F32, name="y_bank")
+        nc.tensor.transpose(b_bank[:], b_rows[:], ident[:])
+        nc.scalar.activation(b_cols[:], b_bank[:, 0:TILES], IDENTITY)
+
+        x_codes = [held("x_codes%d" % a, [P, S], U32) for a in range(PASSES)]
+        x_scales = [held("x_scales%d" % a, [P, S], U8) for a in range(PASSES)]
+        d_codes = [held("d_codes%d" % a, [P, R], U32) for a in range(PASSES)]
+        d_scales = [held("d_scales%d" % a, [P, R], U8) for a in range(PASSES)]
+        u_codes = [held("u_codes%d" % u, [P, UP_CHUNK], U32) for u in range(M // UP_CHUNK)]
+        u_scales = [held("u_scales%d" % u, [P, UP_CHUNK], U8) for u in range(M // UP_CHUNK)]
+        h_codes = held("h_codes", [P, S], U32)
+        h_scales = held("h_scales", [P, S], U8)
+        h_banks = [h_psum.tile([P, PACK, QUARTER], F32, name="h_bank%d" % q) for q in range(4)]
+
+        def quantise(codes, scales, woven):
+            nc.vector.quantize_mx(out=codes.bitcast(FP8X4), scales=scales, in_=woven)
+
+        scalar_copy, vector_copy = nc.scalar.copy, nc.vector.tensor_copy
+
+        def weave(name, raw, width, copy):
+            woven = held(name, [P, PACK * width], BF16)
+            copy(
+                out=woven[:].rearrange("p (c n i) -> p c i n", n=4, i=PACK),
+                in_=raw[:].rearrange("p i (c n) -> p c i n", n=4),
+            )
+            return woven
+
+        def gather(a, lo, hi):
+            picked = held("picked_%d_%d" % (a, lo), [P, PACK, hi - lo], F32)
+            for i in range(PACK):
+                nc.vector.tensor_tensor(
+                    picked[:, i, :], x_planes[a][i][:].indirect(picks[:, lo // 16 : hi // 16]), wgt_sb[:, lo:hi], MULT
+                )
+            return picked
+
+        def make_x(a, lo, hi, picked, copy):
+            woven = weave("x_woven_%d_%d" % (a, lo), picked, hi - lo, copy)
+            quantise(x_codes[a][:, lo:hi], x_scales[a][:, lo:hi], woven[:])
+
+        def make_down(a, shares):
+            woven = held("down_woven%d" % a, [P, PACK * R], BF16)
+            for copy, lo, hi in shares:
+                copy(
+                    out=woven[:].rearrange("p (t m i) -> p m i t", t=PACK, i=PACK)[:, lo:hi],
+                    in_=down_raw[a][:].rearrange("p i (m t) -> p m i t", t=PACK)[:, lo:hi],
+                )
+            quantise(d_codes[a][:], d_scales[a][:], woven[:])
+
+        def make_up(u, copy):
+            woven = weave("up_woven%d" % u, up_raw[u], UP_CHUNK, copy)
+            quantise(u_codes[u][:], u_scales[u][:], woven[:])
+
+        def h_pass(a, q, t):
+            rows, cols = slice(t * P, (t + 1) * P), slice(q * QUARTER, (q + 1) * QUARTER)
+            nc.tensor.matmul_mx(
+                out=h_banks[q][:, t, :],
+                lhsT=d_codes[a][:, rows].bitcast(FP8X4),
+                lhsT_scale=d_scales[a][:, rows],
+                rhs=x_codes[a][:, cols].bitcast(FP8X4),
+                rhs_scale=x_scales[a][:, cols],
+                start=(a == 0 and t == 0),
+                stop=(a == PASSES - 1 and t == PACK - 1),
+            )
+
+        def make_h(half, copies):
+            woven = held("h_woven%d" % half, [P, PACK * HALF], BF16)
+            for n, copy in enumerate(copies):
+                copy(
+                    out=woven[:, n * PACK * QUARTER : (n + 1) * PACK * QUARTER].rearrange("p (n t) -> p n t", t=PACK),
+                    in_=h_banks[2 * half + n][:].rearrange("p t n -> p n t"),
+                )
+            cols = slice(half * HALF, (half + 1) * HALF)
+            quantise(h_codes[:, cols], h_scales[:, cols], woven[:])
+
+        def w4_passes(c, lo, hi):
+            bank = y_psum.tile([P, hi - lo], F32, name="y_bank")
+            words, first = (w4_early, 0) if c < EARLY else (w4_late, EARLY)
+            step = S if hi - lo == S else QUARTER
+            for a in range(PASSES):
+                for n in range(lo, hi, step):
+                    nc.tensor.matmul_mx(
+                        out=bank[:, n - lo : n - lo + step],
+                        lhsT=words[:, a, 2 * P * (c - first) : 2 * P * (c - first + 1)].bitcast(FP4X4),
+                        lhsT_scale=w4_plane[:, a, c * P : (c + 1) * P],
+                        rhs=x_codes[a][:, n : n + step].bitcast(FP8X4),
+                        rhs_scale=x_scales[a][:, n : n + step],
+                        start=(a == 0 and n == lo),
+                        stop=False,
+                    )
+            return bank
+
+        def finish(c, lo, hi, bank):
+            u, col = divmod(c * P, UP_CHUNK)
+            nc.tensor.matmul_mx(
+                out=bank[:],
+                lhsT=u_codes[u][:, col : col + P].bitcast(FP8X4),
+                lhsT_scale=u_scales[u][:, col : col + P],
+                rhs=h_codes[:, lo:hi].bitcast(FP8X4),
+                rhs_scale=h_scales[:, lo:hi],
+                start=False,
+                stop=True,
+            )
+            y = ring.tile([P, hi - lo], F32, name="y", align_bytes=64)
+            nc.scalar.activation(y[:], bank[:], IDENTITY, bias=b_cols[:, c : c + 1])
+            nc.vector.tensor_tensor(
+                pages[c % PAGES][:].indirect(places[:, lo // 16 : hi // 16]), y[:], wgo_sb[:, lo:hi], MULT
+            )
+
+        def store(c):
+            nc.sync.dma_start(out=out[c * P : (c + 1) * P, :], in_=pages[c % PAGES][:])
+
+        last = PASSES - 1
+        for a in range(last):
+            picked = gather(a, 0, S)
+            make_x(a, 0, S, picked, vector_copy if a == 0 else scalar_copy)
+            make_down(a, [(scalar_copy, 0, P)])
+            for t in range(PACK):
+                for q in range(4):
+                    h_pass(a, q, t)
+        halves = [(0, HALF), (HALF, S)]
+        picked = [gather(last, lo, hi) for lo, hi in halves]
+        make_x(last, 0, HALF, picked[0], scalar_copy)
+        make_down(last, [(scalar_copy, 0, DOWN_SPLIT), (vector_copy, DOWN_SPLIT, P)])
+        make_x(last, HALF, S, picked[1], scalar_copy)
+        make_up(0, vector_copy)
+        for half, (lo, hi) in enumerate(halves):
+            for q in (2 * half, 2 * half + 1):
+                for t in range(PACK):
+                    h_pass(last, q, t)
+            banks = [w4_passes(c, lo, hi) for c in range(EARLY)]
+            make_h(half, [vector_copy, scalar_copy] if half == 0 else [scalar_copy, scalar_copy])
+            for c in range(EARLY):
+                finish(c, lo, hi, banks[c])
+        for c in range(EARLY):
+            store(c)
+        for c in range(EARLY, TILES):
+            if c * P % UP_CHUNK == 0:
+                make_up(c * P // UP_CHUNK, scalar_copy)
+            finish(c, 0, S, w4_passes(c, 0, S))
+            store(c)

@@ -25,16 +25,17 @@ HALF = S // 2
 QUARTER = S // 4
 TILES = M // P
 UP_CHUNK = 256
-EARLY = 2
+EARLY = 1
+W4_EARLY = 2
 PAGES = 3
-DOWN_SPLIT = 40
+DOWN_SPLIT = 96
 
 
 def tile_list_hboth_l_bias_kernel(tc, xT, w4_words, w4_scales, down, up, wgt, b, wgo, offs, offs2, out):
     nc = tc.nc
     with ExitStack() as ctx:
         keep = ctx.enter_context(tc.tile_pool(name="keep", bufs=1))
-        ring = ctx.enter_context(tc.tile_pool(name="ring", bufs=3))
+        ring = ctx.enter_context(tc.tile_pool(name="ring", bufs=4))
         h_psum = ctx.enter_context(tc.psum_pool(name="h_psum", bufs=1))
         y_psum = ctx.enter_context(tc.psum_pool(name="y_psum", bufs=4))
 
@@ -48,7 +49,7 @@ def tile_list_hboth_l_bias_kernel(tc, xT, w4_words, w4_scales, down, up, wgt, b,
         x_planes = [[held("x_%d_%d" % (a, i), [P, T], F32) for i in range(PACK)] for a in range(PASSES)]
         down_raw = [held("down_raw%d" % a, [P, PACK, R], F32) for a in range(PASSES)]
         up_raw = [held("up_raw%d" % u, [P, PACK, UP_CHUNK], F32) for u in range(M // UP_CHUNK)]
-        early_cols = EARLY * P
+        early_cols = W4_EARLY * P
         w4_early = held("w4_early", [P, PASSES, 2 * early_cols], U8)
         w4_late = held("w4_late", [P, PASSES, 2 * (M - early_cols)], U8)
         w4_plane = held("w4_plane", [P, PASSES, M], U8)
@@ -62,12 +63,12 @@ def tile_list_hboth_l_bias_kernel(tc, xT, w4_words, w4_scales, down, up, wgt, b,
         up_rows = up.rearrange("(p i) n -> p i n", i=PACK)
         w4_rows = w4_words.rearrange("a p n -> p a n")
 
-        make_identity(nc, ident[:])
         nc.gpsimd.memset(b_rows[:], 0.0)
-        nc.gpsimd.dma_start(out=b_rows[0:TILES, :], in_=b.rearrange("(c p) -> c p", p=P))
+        make_identity(nc, ident[:])
+        nc.scalar.dma_start(out=b_rows[0:TILES, :], in_=b.rearrange("(c p) -> c p", p=P))
         nc.vector.memset(w4_plane[:].rearrange("p a n -> p (a n)").bitcast(I32), 0)
         for q in range(4):
-            nc.gpsimd.dma_start(
+            nc.scalar.dma_start(
                 out=w4_plane[32 * q : 32 * q + 4, :, :].bitcast(I32),
                 in_=w4_scales[:, 4 * q : 4 * q + 4, :].rearrange("a r n -> r a n").bitcast(I32),
             )
@@ -79,20 +80,19 @@ def tile_list_hboth_l_bias_kernel(tc, xT, w4_words, w4_scales, down, up, wgt, b,
         nc.sync.dma_start(out=wgt_sb[:], in_=wgt)
         for i in range(1, PACK):
             nc.sync.dma_start(out=x_planes[0][i][:], in_=x_rows[0, i])
-        nc.sync.dma_start(out=down_raw[0][:], in_=down_rows[0])
-        for i in range(PACK):
-            nc.sync.dma_start(out=x_planes[1][i][:], in_=x_rows[1, i])
-        nc.sync.dma_start(out=down_raw[1][:], in_=down_rows[1])
-        for i in range(PACK):
-            nc.sync.dma_start(out=x_planes[2][i][:], in_=x_rows[2, i])
+        planes = [(a, i) for a in range(1, PASSES) for i in range(PACK)]
+        down_before = {(1, 2): 0, (2, 2): 1}
+        for a, i in planes:
+            if (a, i) in down_before:
+                nc.sync.dma_start(out=down_raw[down_before[a, i]][:], in_=down_rows[down_before[a, i]])
+            nc.sync.dma_start(out=x_planes[a][i][:], in_=x_rows[a, i])
         nc.sync.dma_start(out=down_raw[2][:], in_=down_rows[2])
-        nc.sync.dma_start(out=up_raw[0][:], in_=up_rows[:, :, 0:UP_CHUNK])
         nc.sync.dma_start(out=w4_early[:].bitcast(I32), in_=w4_rows[:, :, 0 : 2 * early_cols].bitcast(I32))
+        nc.sync.dma_start(out=up_raw[0][:], in_=up_rows[:, :, 0:UP_CHUNK])
         nc.sync.dma_start(out=wgo_sb[:], in_=wgo)
         nc.sync.dma_start(places[:], offs2)
-        nc.sync.dma_start(out=up_raw[1][:], in_=up_rows[:, :, UP_CHUNK : 2 * UP_CHUNK])
         nc.sync.dma_start(out=w4_late[:].bitcast(I32), in_=w4_rows[:, :, 2 * early_cols :].bitcast(I32))
-        for u in range(2, M // UP_CHUNK):
+        for u in range(1, M // UP_CHUNK):
             nc.sync.dma_start(out=up_raw[u][:], in_=up_rows[:, :, u * UP_CHUNK : (u + 1) * UP_CHUNK])
 
         b_bank = y_psum.tile([P, P], F32, name="y_bank")
@@ -144,7 +144,7 @@ def tile_list_hboth_l_bias_kernel(tc, xT, w4_words, w4_scales, down, up, wgt, b,
             quantise(d_codes[a][:], d_scales[a][:], woven[:])
 
         def make_up(u, copy):
-            woven = weave("up_woven%d" % u, up_raw[u], UP_CHUNK, copy)
+            woven = weave("late_woven" if u else "up_woven", up_raw[u], UP_CHUNK, copy)
             quantise(u_codes[u][:], u_scales[u][:], woven[:])
 
         def h_pass(a, q, t):
@@ -160,7 +160,7 @@ def tile_list_hboth_l_bias_kernel(tc, xT, w4_words, w4_scales, down, up, wgt, b,
             )
 
         def make_h(half, copies):
-            woven = held("h_woven%d" % half, [P, PACK * HALF], BF16)
+            woven = held("late_woven" if half else "h_woven", [P, PACK * HALF], BF16)
             for n, copy in enumerate(copies):
                 copy(
                     out=woven[:, n * PACK * QUARTER : (n + 1) * PACK * QUARTER].rearrange("p (n t) -> p n t", t=PACK),
@@ -171,7 +171,7 @@ def tile_list_hboth_l_bias_kernel(tc, xT, w4_words, w4_scales, down, up, wgt, b,
 
         def w4_passes(c, lo, hi):
             bank = y_psum.tile([P, hi - lo], F32, name="y_bank")
-            words, first = (w4_early, 0) if c < EARLY else (w4_late, EARLY)
+            words, first = (w4_early, 0) if c < W4_EARLY else (w4_late, W4_EARLY)
             step = S if hi - lo == S else QUARTER
             for a in range(PASSES):
                 for n in range(lo, hi, step):
@@ -207,30 +207,23 @@ def tile_list_hboth_l_bias_kernel(tc, xT, w4_words, w4_scales, down, up, wgt, b,
             nc.sync.dma_start(out=out[c * P : (c + 1) * P, :], in_=pages[c % PAGES][:])
 
         last = PASSES - 1
-        for a in range(last):
-            picked = gather(a, 0, S)
-            make_x(a, 0, S, picked, vector_copy if a == 0 else scalar_copy)
-            make_down(a, [(scalar_copy, 0, P)])
-            for t in range(PACK):
-                for q in range(4):
-                    h_pass(a, q, t)
-        halves = [(0, HALF), (HALF, S)]
-        picked = [gather(last, lo, hi) for lo, hi in halves]
-        make_x(last, 0, HALF, picked[0], scalar_copy)
-        make_down(last, [(scalar_copy, 0, DOWN_SPLIT), (vector_copy, DOWN_SPLIT, P)])
-        make_x(last, HALF, S, picked[1], scalar_copy)
-        make_up(0, vector_copy)
-        for half, (lo, hi) in enumerate(halves):
+        for a in range(PASSES):
+            make_x(a, 0, S, gather(a, 0, S), vector_copy if a == last else scalar_copy)
+            make_down(a, [(scalar_copy, 0, DOWN_SPLIT), (vector_copy, DOWN_SPLIT, P)] if a == last else [(scalar_copy, 0, P)])
+            if a < last:
+                for t in range(PACK):
+                    for q in range(4):
+                        h_pass(a, q, t)
+        make_up(0, scalar_copy)
+        for half, (lo, hi) in enumerate([(0, HALF), (HALF, S)]):
             for q in (2 * half, 2 * half + 1):
                 for t in range(PACK):
                     h_pass(last, q, t)
-            banks = [w4_passes(c, lo, hi) for c in range(EARLY)]
-            make_h(half, [vector_copy, scalar_copy] if half == 0 else [scalar_copy, scalar_copy])
-            for c in range(EARLY):
-                finish(c, lo, hi, banks[c])
-        for c in range(EARLY):
-            store(c)
-        for c in range(EARLY, TILES):
+            bank = w4_passes(0, lo, hi)
+            make_h(half, [vector_copy, scalar_copy])
+            finish(0, lo, hi, bank)
+        store(0)
+        for c in range(1, TILES):
             if c * P % UP_CHUNK == 0:
                 make_up(c * P // UP_CHUNK, scalar_copy)
             finish(c, 0, S, w4_passes(c, 0, S))

@@ -28,7 +28,6 @@ UP_CHUNK = 256
 EARLY = 1
 W4_EARLY = 2
 PAGES = 3
-DOWN_SPLIT = 96
 
 
 def tile_list_hboth_l_bias_kernel(tc, xT, w4_words, w4_scales, down, up, wgt, b, wgo, offs, offs2, out):
@@ -37,7 +36,7 @@ def tile_list_hboth_l_bias_kernel(tc, xT, w4_words, w4_scales, down, up, wgt, b,
         keep = ctx.enter_context(tc.tile_pool(name="keep", bufs=1))
         ring = ctx.enter_context(tc.tile_pool(name="ring", bufs=4))
         h_psum = ctx.enter_context(tc.psum_pool(name="h_psum", bufs=1))
-        y_psum = ctx.enter_context(tc.psum_pool(name="y_psum", bufs=4))
+        y_psum = ctx.enter_context(tc.psum_pool(name="y_psum", bufs=2))
 
         def held(name, shape, dtype):
             return keep.tile(shape, dtype, name=name, align_bytes=64)
@@ -52,7 +51,8 @@ def tile_list_hboth_l_bias_kernel(tc, xT, w4_words, w4_scales, down, up, wgt, b,
         early_cols = W4_EARLY * P
         w4_early = held("w4_early", [P, PASSES, 2 * early_cols], U8)
         w4_late = held("w4_late", [P, PASSES, 2 * (M - early_cols)], U8)
-        w4_plane = held("w4_plane", [P, PASSES, M], U8)
+        plane_early = held("plane_early", [P, PASSES, early_cols], U8)
+        plane_late = held("plane_late", [P, PASSES, M - early_cols], U8)
         b_rows = held("b_rows", [P, P], F32)
         ident = held("ident", [P, P], F32)
         b_cols = held("b_cols", [P, TILES], F32)
@@ -66,12 +66,17 @@ def tile_list_hboth_l_bias_kernel(tc, xT, w4_words, w4_scales, down, up, wgt, b,
         nc.gpsimd.memset(b_rows[:], 0.0)
         make_identity(nc, ident[:])
         nc.scalar.dma_start(out=b_rows[0:TILES, :], in_=b.rearrange("(c p) -> c p", p=P))
-        nc.vector.memset(w4_plane[:].rearrange("p a n -> p (a n)").bitcast(I32), 0)
-        for q in range(4):
-            nc.scalar.dma_start(
-                out=w4_plane[32 * q : 32 * q + 4, :, :].bitcast(I32),
-                in_=w4_scales[:, 4 * q : 4 * q + 4, :].rearrange("a r n -> r a n").bitcast(I32),
-            )
+        for plane in (plane_early, plane_late):
+            nc.vector.memset(plane[:].rearrange("p a n -> p (a n)").bitcast(I32), 0)
+
+        def load_plane(queue, plane, cols):
+            for q in range(4):
+                queue.dma_start(
+                    out=plane[32 * q : 32 * q + 4, :, :].bitcast(I32),
+                    in_=w4_scales[:, 4 * q : 4 * q + 4, cols].rearrange("a r n -> r a n").bitcast(I32),
+                )
+
+        load_plane(nc.scalar, plane_early, slice(0, early_cols))
         for page in pages:
             nc.vector.memset(page[:], 0.0)
 
@@ -81,16 +86,16 @@ def tile_list_hboth_l_bias_kernel(tc, xT, w4_words, w4_scales, down, up, wgt, b,
         for i in range(1, PACK):
             nc.sync.dma_start(out=x_planes[0][i][:], in_=x_rows[0, i])
         planes = [(a, i) for a in range(1, PASSES) for i in range(PACK)]
-        down_before = {(1, 2): 0, (2, 2): 1}
+        down_before = {(1, 2): 0, (2, 1): 1, (2, 3): 2}
         for a, i in planes:
             if (a, i) in down_before:
                 nc.sync.dma_start(out=down_raw[down_before[a, i]][:], in_=down_rows[down_before[a, i]])
             nc.sync.dma_start(out=x_planes[a][i][:], in_=x_rows[a, i])
-        nc.sync.dma_start(out=down_raw[2][:], in_=down_rows[2])
         nc.sync.dma_start(out=w4_early[:].bitcast(I32), in_=w4_rows[:, :, 0 : 2 * early_cols].bitcast(I32))
         nc.sync.dma_start(out=up_raw[0][:], in_=up_rows[:, :, 0:UP_CHUNK])
         nc.sync.dma_start(out=wgo_sb[:], in_=wgo)
         nc.sync.dma_start(places[:], offs2)
+        load_plane(nc.sync, plane_late, slice(early_cols, M))
         nc.sync.dma_start(out=w4_late[:].bitcast(I32), in_=w4_rows[:, :, 2 * early_cols :].bitcast(I32))
         for u in range(1, M // UP_CHUNK):
             nc.sync.dma_start(out=up_raw[u][:], in_=up_rows[:, :, u * UP_CHUNK : (u + 1) * UP_CHUNK])
@@ -99,9 +104,8 @@ def tile_list_hboth_l_bias_kernel(tc, xT, w4_words, w4_scales, down, up, wgt, b,
         nc.tensor.transpose(b_bank[:], b_rows[:], ident[:])
         nc.scalar.activation(b_cols[:], b_bank[:, 0:TILES], IDENTITY)
 
-        x_codes = [held("x_codes%d" % a, [P, S], U32) for a in range(PASSES)]
+        x_codes, d_codes = [], []
         x_scales = [held("x_scales%d" % a, [P, S], U8) for a in range(PASSES)]
-        d_codes = [held("d_codes%d" % a, [P, R], U32) for a in range(PASSES)]
         d_scales = [held("d_scales%d" % a, [P, R], U8) for a in range(PASSES)]
         u_codes = [held("u_codes%d" % u, [P, UP_CHUNK], U32) for u in range(M // UP_CHUNK)]
         u_scales = [held("u_scales%d" % u, [P, UP_CHUNK], U8) for u in range(M // UP_CHUNK)]
@@ -118,33 +122,25 @@ def tile_list_hboth_l_bias_kernel(tc, xT, w4_words, w4_scales, down, up, wgt, b,
             woven = held(name, [P, PACK * width], BF16)
             copy(
                 out=woven[:].rearrange("p (c n i) -> p c i n", n=4, i=PACK),
-                in_=raw[:].rearrange("p i (c n) -> p c i n", n=4),
+                in_=raw.rearrange("p i (c n) -> p c i n", n=4),
             )
             return woven
 
-        def gather(a, lo, hi):
-            picked = held("picked_%d_%d" % (a, lo), [P, PACK, hi - lo], F32)
-            for i in range(PACK):
-                nc.vector.tensor_tensor(
-                    picked[:, i, :], x_planes[a][i][:].indirect(picks[:, lo // 16 : hi // 16]), wgt_sb[:, lo:hi], MULT
-                )
-            return picked
+        def gather(a, i, picked, lo, hi):
+            nc.vector.tensor_tensor(
+                picked[:, i, :], x_planes[a][i][:].indirect(picks[:, lo // 16 : hi // 16]), wgt_sb[:, lo:hi], MULT
+            )
 
-        def make_x(a, lo, hi, picked, copy):
-            woven = weave("x_woven_%d_%d" % (a, lo), picked, hi - lo, copy)
-            quantise(x_codes[a][:, lo:hi], x_scales[a][:, lo:hi], woven[:])
-
-        def make_down(a, shares):
+        def weave_down(a):
             woven = held("down_woven%d" % a, [P, PACK * R], BF16)
-            for copy, lo, hi in shares:
-                copy(
-                    out=woven[:].rearrange("p (t m i) -> p m i t", t=PACK, i=PACK)[:, lo:hi],
-                    in_=down_raw[a][:].rearrange("p i (m t) -> p m i t", t=PACK)[:, lo:hi],
-                )
-            quantise(d_codes[a][:], d_scales[a][:], woven[:])
+            nc.scalar.copy(
+                out=woven[:].rearrange("p (t m i) -> p m i t", t=PACK, i=PACK),
+                in_=down_raw[a][:].rearrange("p i (m t) -> p m i t", t=PACK),
+            )
+            return woven
 
         def make_up(u, copy):
-            woven = weave("late_woven" if u else "up_woven", up_raw[u], UP_CHUNK, copy)
+            woven = weave("late_woven" if u else "up_woven", up_raw[u][:], UP_CHUNK, copy)
             quantise(u_codes[u][:], u_scales[u][:], woven[:])
 
         def h_pass(a, q, t):
@@ -171,14 +167,14 @@ def tile_list_hboth_l_bias_kernel(tc, xT, w4_words, w4_scales, down, up, wgt, b,
 
         def w4_passes(c, lo, hi):
             bank = y_psum.tile([P, hi - lo], F32, name="y_bank")
-            words, first = (w4_early, 0) if c < W4_EARLY else (w4_late, W4_EARLY)
+            words, plane, first = (w4_early, plane_early, 0) if c < W4_EARLY else (w4_late, plane_late, W4_EARLY)
             step = S if hi - lo == S else QUARTER
             for a in range(PASSES):
                 for n in range(lo, hi, step):
                     nc.tensor.matmul_mx(
                         out=bank[:, n - lo : n - lo + step],
                         lhsT=words[:, a, 2 * P * (c - first) : 2 * P * (c - first + 1)].bitcast(FP4X4),
-                        lhsT_scale=w4_plane[:, a, c * P : (c + 1) * P],
+                        lhsT_scale=plane[:, a, P * (c - first) : P * (c - first + 1)],
                         rhs=x_codes[a][:, n : n + step].bitcast(FP8X4),
                         rhs_scale=x_scales[a][:, n : n + step],
                         start=(a == 0 and n == lo),
@@ -207,15 +203,37 @@ def tile_list_hboth_l_bias_kernel(tc, xT, w4_words, w4_scales, down, up, wgt, b,
             nc.sync.dma_start(out=out[c * P : (c + 1) * P, :], in_=pages[c % PAGES][:])
 
         last = PASSES - 1
+        halves = [(0, HALF), (HALF, S)]
+        x_woven = down_woven = None
         for a in range(PASSES):
-            make_x(a, 0, S, gather(a, 0, S), vector_copy if a == last else scalar_copy)
-            make_down(a, [(scalar_copy, 0, DOWN_SPLIT), (vector_copy, DOWN_SPLIT, P)] if a == last else [(scalar_copy, 0, P)])
+            parts = halves if a == last else [(0, S)]
+            picked = [held("picked_%d_%d" % (a, lo), [P, PACK, hi - lo], F32) for lo, hi in parts]
+            for i in range(PACK):
+                for part, (lo, hi) in zip(picked, parts):
+                    gather(a, i, part, lo, hi)
+                if a > 0 and i == 1:
+                    x_codes.append(held("x_%d_%d" % (a, i), [P, S], U32))
+                    quantise(x_codes[a - 1][:], x_scales[a - 1][:], x_woven[:])
+                if a > 0 and i == PACK - a:
+                    d_codes.append(held("x_%d_%d" % (a, i), [P, R], U32))
+                    quantise(d_codes[a - 1][:], d_scales[a - 1][:], down_woven[:])
+                    for t in range(PACK):
+                        for q in range(4):
+                            h_pass(a - 1, q, t)
             if a < last:
-                for t in range(PACK):
-                    for q in range(4):
-                        h_pass(a, q, t)
-        make_up(0, scalar_copy)
-        for half, (lo, hi) in enumerate([(0, HALF), (HALF, S)]):
+                x_woven = weave("x_woven%d" % a, picked[0][:], S, scalar_copy)
+            down_woven = weave_down(a)
+        x_codes.append(held("x_codes_last", [P, S], U32))
+        d_codes.append(held("d_codes_last", [P, R], U32))
+        x_woven = [
+            weave("x_woven_last%d" % n, part[:], HALF, copy)
+            for n, (part, copy) in enumerate(zip(picked, (vector_copy, scalar_copy)))
+        ]
+        quantise(d_codes[last][:], d_scales[last][:], down_woven[:])
+        for half, (lo, hi) in enumerate(halves):
+            quantise(x_codes[last][:, lo:hi], x_scales[last][:, lo:hi], x_woven[half][:])
+            if half == 0:
+                make_up(0, scalar_copy)
             for q in (2 * half, 2 * half + 1):
                 for t in range(PACK):
                     h_pass(last, q, t)

@@ -19,40 +19,47 @@ IDENTITY = mybir.ActivationFunctionType.Identity
 
 P = 128
 PACK = 4
-K_PASS = P * PACK
-PASSES = K // K_PASS
+PASSES = K // (P * PACK)
+LAST = PASSES - 1
+GROUP = 16
+LINE = 4
+QUADRANTS = 4
 HALF = S // 2
-QUARTER = S // 4
+QUARTER = S // PACK
+HALVES = ((0, HALF), (HALF, S))
 TILES = M // P
-UP_CHUNK = 256
-EARLY = 1
-W4_EARLY = 2
+UP_CHUNK = 2 * P
+CHUNKS = M // UP_CHUNK
+EARLY_COLS = UP_CHUNK
 PAGES = 3
+Y_BANKS = 2
+Y_TILES = 4
+DOWN_BEFORE = (6, 9, PASSES * PACK - 1)
 
 
 def tile_list_hboth_l_bias_kernel(tc, xT, w4_words, w4_scales, down, up, wgt, b, wgo, offs, offs2, out):
     nc = tc.nc
+    scalar_copy, vector_copy = nc.scalar.copy, nc.vector.tensor_copy
     with ExitStack() as ctx:
         keep = ctx.enter_context(tc.tile_pool(name="keep", bufs=1))
-        ring = ctx.enter_context(tc.tile_pool(name="ring", bufs=4))
+        y_pool = ctx.enter_context(tc.tile_pool(name="y_pool", bufs=Y_TILES))
         h_psum = ctx.enter_context(tc.psum_pool(name="h_psum", bufs=1))
-        y_psum = ctx.enter_context(tc.psum_pool(name="y_psum", bufs=2))
+        y_psum = ctx.enter_context(tc.psum_pool(name="y_psum", bufs=Y_BANKS))
 
         def held(name, shape, dtype):
             return keep.tile(shape, dtype, name=name, align_bytes=64)
 
-        picks = keep.tile([P, S // 16], U16, name="picks")
-        places = keep.tile([P, S // 16], U16, name="places")
+        picks = keep.tile([P, S // GROUP], U16, name="picks")
+        places = keep.tile([P, S // GROUP], U16, name="places")
         wgt_sb = held("wgt_sb", [P, S], F32)
         wgo_sb = held("wgo_sb", [P, S], F32)
-        x_planes = [[held("x_%d_%d" % (a, i), [P, T], F32) for i in range(PACK)] for a in range(PASSES)]
+        x_planes = [held("plane%d" % n, [P, T], F32) for n in range(PASSES * PACK)]
         down_raw = [held("down_raw%d" % a, [P, PACK, R], F32) for a in range(PASSES)]
-        up_raw = [held("up_raw%d" % u, [P, PACK, UP_CHUNK], F32) for u in range(M // UP_CHUNK)]
-        early_cols = W4_EARLY * P
-        w4_early = held("w4_early", [P, PASSES, 2 * early_cols], U8)
-        w4_late = held("w4_late", [P, PASSES, 2 * (M - early_cols)], U8)
-        plane_early = held("plane_early", [P, PASSES, early_cols], U8)
-        plane_late = held("plane_late", [P, PASSES, M - early_cols], U8)
+        up_raw = [held("up_raw%d" % u, [P, PACK, UP_CHUNK], F32) for u in range(CHUNKS)]
+        w4_early = held("w4_early", [P, PASSES, 2 * EARLY_COLS], U8)
+        w4_late = held("w4_late", [P, PASSES, 2 * (M - EARLY_COLS)], U8)
+        w4_scales_early = held("w4_scales_early", [P, PASSES, EARLY_COLS], U8)
+        w4_scales_late = held("w4_scales_late", [P, PASSES, M - EARLY_COLS], U8)
         b_rows = held("b_rows", [P, P], F32)
         ident = held("ident", [P, P], F32)
         b_cols = held("b_cols", [P, TILES], F32)
@@ -63,121 +70,128 @@ def tile_list_hboth_l_bias_kernel(tc, xT, w4_words, w4_scales, down, up, wgt, b,
         up_rows = up.rearrange("(p i) n -> p i n", i=PACK)
         w4_rows = w4_words.rearrange("a p n -> p a n")
 
+        def load_scales(queue, scales, cols):
+            for quad in range(QUADRANTS):
+                queue.dma_start(
+                    out=scales[32 * quad : 32 * quad + 4, :, :].bitcast(I32),
+                    in_=w4_scales[:, 4 * quad : 4 * quad + 4, cols].rearrange("a r n -> r a n").bitcast(I32),
+                )
+
+        def load_plane(n):
+            nc.sync.dma_start(out=x_planes[n][:], in_=x_rows[n // PACK, n % PACK])
+
+        def load_up(u):
+            nc.sync.dma_start(out=up_raw[u][:], in_=up_rows[:, :, u * UP_CHUNK : (u + 1) * UP_CHUNK])
+
         nc.gpsimd.memset(b_rows[:], 0.0)
         make_identity(nc, ident[:])
         nc.scalar.dma_start(out=b_rows[0:TILES, :], in_=b.rearrange("(c p) -> c p", p=P))
-        for plane in (plane_early, plane_late):
-            nc.vector.memset(plane[:].rearrange("p a n -> p (a n)").bitcast(I32), 0)
-
-        def load_plane(queue, plane, cols):
-            for q in range(4):
-                queue.dma_start(
-                    out=plane[32 * q : 32 * q + 4, :, :].bitcast(I32),
-                    in_=w4_scales[:, 4 * q : 4 * q + 4, cols].rearrange("a r n -> r a n").bitcast(I32),
-                )
-
-        load_plane(nc.scalar, plane_early, slice(0, early_cols))
+        for scales in (w4_scales_early, w4_scales_late):
+            nc.vector.memset(scales[:].rearrange("p a n -> p (a n)").bitcast(I32), 0)
+        load_scales(nc.scalar, w4_scales_early, slice(0, EARLY_COLS))
         for page in pages:
             nc.vector.memset(page[:], 0.0)
 
         nc.sync.dma_start(picks[:], offs)
-        nc.sync.dma_start(out=x_planes[0][0][:], in_=x_rows[0, 0])
+        load_plane(0)
         nc.sync.dma_start(out=wgt_sb[:], in_=wgt)
-        for i in range(1, PACK):
-            nc.sync.dma_start(out=x_planes[0][i][:], in_=x_rows[0, i])
-        planes = [(a, i) for a in range(1, PASSES) for i in range(PACK)]
-        down_before = {(1, 2): 0, (2, 1): 1, (2, 3): 2}
-        for a, i in planes:
-            if (a, i) in down_before:
-                nc.sync.dma_start(out=down_raw[down_before[a, i]][:], in_=down_rows[down_before[a, i]])
-            nc.sync.dma_start(out=x_planes[a][i][:], in_=x_rows[a, i])
-        nc.sync.dma_start(out=w4_early[:].bitcast(I32), in_=w4_rows[:, :, 0 : 2 * early_cols].bitcast(I32))
-        nc.sync.dma_start(out=up_raw[0][:], in_=up_rows[:, :, 0:UP_CHUNK])
+        for n in range(1, PASSES * PACK):
+            if n in DOWN_BEFORE:
+                a = DOWN_BEFORE.index(n)
+                nc.sync.dma_start(out=down_raw[a][:], in_=down_rows[a])
+            load_plane(n)
+        nc.sync.dma_start(out=w4_early[:].bitcast(I32), in_=w4_rows[:, :, 0 : 2 * EARLY_COLS].bitcast(I32))
+        load_up(0)
         nc.sync.dma_start(out=wgo_sb[:], in_=wgo)
         nc.sync.dma_start(places[:], offs2)
-        load_plane(nc.sync, plane_late, slice(early_cols, M))
-        nc.sync.dma_start(out=w4_late[:].bitcast(I32), in_=w4_rows[:, :, 2 * early_cols :].bitcast(I32))
-        for u in range(1, M // UP_CHUNK):
-            nc.sync.dma_start(out=up_raw[u][:], in_=up_rows[:, :, u * UP_CHUNK : (u + 1) * UP_CHUNK])
+        load_scales(nc.sync, w4_scales_late, slice(EARLY_COLS, M))
+        nc.sync.dma_start(out=w4_late[:].bitcast(I32), in_=w4_rows[:, :, 2 * EARLY_COLS :].bitcast(I32))
+        for u in range(1, CHUNKS):
+            load_up(u)
 
         b_bank = y_psum.tile([P, P], F32, name="y_bank")
         nc.tensor.transpose(b_bank[:], b_rows[:], ident[:])
         nc.scalar.activation(b_cols[:], b_bank[:, 0:TILES], IDENTITY)
 
-        x_codes, d_codes = [], []
+        x_codes, down_codes = [], []
         x_scales = [held("x_scales%d" % a, [P, S], U8) for a in range(PASSES)]
-        d_scales = [held("d_scales%d" % a, [P, R], U8) for a in range(PASSES)]
-        u_codes = [held("u_codes%d" % u, [P, UP_CHUNK], U32) for u in range(M // UP_CHUNK)]
-        u_scales = [held("u_scales%d" % u, [P, UP_CHUNK], U8) for u in range(M // UP_CHUNK)]
+        down_scales = [held("down_scales%d" % a, [P, R], U8) for a in range(PASSES)]
+        up_codes = [held("up_codes%d" % u, [P, UP_CHUNK], U32) for u in range(CHUNKS)]
+        up_scales = [held("up_scales%d" % u, [P, UP_CHUNK], U8) for u in range(CHUNKS)]
         h_codes = held("h_codes", [P, S], U32)
         h_scales = held("h_scales", [P, S], U8)
-        h_banks = [h_psum.tile([P, PACK, QUARTER], F32, name="h_bank%d" % q) for q in range(4)]
+        h_banks = [h_psum.tile([P, PACK, QUARTER], F32, name="h_bank%d" % q) for q in range(S // QUARTER)]
 
-        def quantise(codes, scales, woven):
-            nc.vector.quantize_mx(out=codes.bitcast(FP8X4), scales=scales, in_=woven)
-
-        scalar_copy, vector_copy = nc.scalar.copy, nc.vector.tensor_copy
+        def gather(n, picked, lo, hi):
+            nc.vector.tensor_tensor(
+                picked[:, n % PACK, lo:hi],
+                x_planes[n][:].indirect(picks[:, lo // GROUP : hi // GROUP]),
+                wgt_sb[:, lo:hi],
+                MULT,
+            )
 
         def weave(name, raw, width, copy):
             woven = held(name, [P, PACK * width], BF16)
             copy(
-                out=woven[:].rearrange("p (c n i) -> p c i n", n=4, i=PACK),
-                in_=raw.rearrange("p i (c n) -> p c i n", n=4),
+                out=woven[:].rearrange("p (c n i) -> p c i n", n=LINE, i=PACK),
+                in_=raw.rearrange("p i (c n) -> p c i n", n=LINE),
             )
             return woven
 
-        def gather(a, i, picked, lo, hi):
-            nc.vector.tensor_tensor(
-                picked[:, i, :], x_planes[a][i][:].indirect(picks[:, lo // 16 : hi // 16]), wgt_sb[:, lo:hi], MULT
-            )
-
         def weave_down(a):
             woven = held("down_woven%d" % a, [P, PACK * R], BF16)
-            nc.scalar.copy(
+            scalar_copy(
                 out=woven[:].rearrange("p (t m i) -> p m i t", t=PACK, i=PACK),
                 in_=down_raw[a][:].rearrange("p i (m t) -> p m i t", t=PACK),
             )
             return woven
 
-        def make_up(u, copy):
-            woven = weave("late_woven" if u else "up_woven", up_raw[u][:], UP_CHUNK, copy)
-            quantise(u_codes[u][:], u_scales[u][:], woven[:])
+        def quantise(codes, scales, woven):
+            nc.vector.quantize_mx(out=codes.bitcast(FP8X4), scales=scales, in_=woven)
+
+        def make_up(u):
+            woven = weave("late_woven" if u else "up_woven", up_raw[u][:], UP_CHUNK, scalar_copy)
+            quantise(up_codes[u][:], up_scales[u][:], woven[:])
 
         def h_pass(a, q, t):
             rows, cols = slice(t * P, (t + 1) * P), slice(q * QUARTER, (q + 1) * QUARTER)
             nc.tensor.matmul_mx(
                 out=h_banks[q][:, t, :],
-                lhsT=d_codes[a][:, rows].bitcast(FP8X4),
-                lhsT_scale=d_scales[a][:, rows],
+                lhsT=down_codes[a][:, rows].bitcast(FP8X4),
+                lhsT_scale=down_scales[a][:, rows],
                 rhs=x_codes[a][:, cols].bitcast(FP8X4),
                 rhs_scale=x_scales[a][:, cols],
                 start=(a == 0 and t == 0),
-                stop=(a == PASSES - 1 and t == PACK - 1),
+                stop=(a == LAST and t == PACK - 1),
             )
 
-        def make_h(half, copies):
+        def make_h(half):
+            lo, hi = HALVES[half]
             woven = held("late_woven" if half else "h_woven", [P, PACK * HALF], BF16)
-            for n, copy in enumerate(copies):
-                copy(
-                    out=woven[:, n * PACK * QUARTER : (n + 1) * PACK * QUARTER].rearrange("p (n t) -> p n t", t=PACK),
-                    in_=h_banks[2 * half + n][:].rearrange("p t n -> p n t"),
+            for q in range(lo // QUARTER, hi // QUARTER):
+                first = PACK * (q * QUARTER - lo)
+                (vector_copy if q == 0 else scalar_copy)(
+                    out=woven[:, first : first + PACK * QUARTER].rearrange("p (n t) -> p n t", t=PACK),
+                    in_=h_banks[q][:].rearrange("p t n -> p n t"),
                 )
-            cols = slice(half * HALF, (half + 1) * HALF)
-            quantise(h_codes[:, cols], h_scales[:, cols], woven[:])
+            quantise(h_codes[:, lo:hi], h_scales[:, lo:hi], woven[:])
 
         def w4_passes(c, lo, hi):
             bank = y_psum.tile([P, hi - lo], F32, name="y_bank")
-            words, plane, first = (w4_early, plane_early, 0) if c < W4_EARLY else (w4_late, plane_late, W4_EARLY)
-            step = S if hi - lo == S else QUARTER
+            if c * P < EARLY_COLS:
+                words, scales, col = w4_early, w4_scales_early, c * P
+            else:
+                words, scales, col = w4_late, w4_scales_late, c * P - EARLY_COLS
+            width = S if hi - lo == S else QUARTER
             for a in range(PASSES):
-                for n in range(lo, hi, step):
+                for j in range(lo, hi, width):
                     nc.tensor.matmul_mx(
-                        out=bank[:, n - lo : n - lo + step],
-                        lhsT=words[:, a, 2 * P * (c - first) : 2 * P * (c - first + 1)].bitcast(FP4X4),
-                        lhsT_scale=plane[:, a, P * (c - first) : P * (c - first + 1)],
-                        rhs=x_codes[a][:, n : n + step].bitcast(FP8X4),
-                        rhs_scale=x_scales[a][:, n : n + step],
-                        start=(a == 0 and n == lo),
+                        out=bank[:, j - lo : j - lo + width],
+                        lhsT=words[:, a, 2 * col : 2 * (col + P)].bitcast(FP4X4),
+                        lhsT_scale=scales[:, a, col : col + P],
+                        rhs=x_codes[a][:, j : j + width].bitcast(FP8X4),
+                        rhs_scale=x_scales[a][:, j : j + width],
+                        start=(a == 0 and j == lo),
                         stop=False,
                     )
             return bank
@@ -186,63 +200,62 @@ def tile_list_hboth_l_bias_kernel(tc, xT, w4_words, w4_scales, down, up, wgt, b,
             u, col = divmod(c * P, UP_CHUNK)
             nc.tensor.matmul_mx(
                 out=bank[:],
-                lhsT=u_codes[u][:, col : col + P].bitcast(FP8X4),
-                lhsT_scale=u_scales[u][:, col : col + P],
+                lhsT=up_codes[u][:, col : col + P].bitcast(FP8X4),
+                lhsT_scale=up_scales[u][:, col : col + P],
                 rhs=h_codes[:, lo:hi].bitcast(FP8X4),
                 rhs_scale=h_scales[:, lo:hi],
                 start=False,
                 stop=True,
             )
-            y = ring.tile([P, hi - lo], F32, name="y", align_bytes=64)
+            y = y_pool.tile([P, hi - lo], F32, name="y", align_bytes=64)
             nc.scalar.activation(y[:], bank[:], IDENTITY, bias=b_cols[:, c : c + 1])
             nc.vector.tensor_tensor(
-                pages[c % PAGES][:].indirect(places[:, lo // 16 : hi // 16]), y[:], wgo_sb[:, lo:hi], MULT
+                pages[c % PAGES][:].indirect(places[:, lo // GROUP : hi // GROUP]), y[:], wgo_sb[:, lo:hi], MULT
             )
 
         def store(c):
             nc.sync.dma_start(out=out[c * P : (c + 1) * P, :], in_=pages[c % PAGES][:])
 
-        last = PASSES - 1
-        halves = [(0, HALF), (HALF, S)]
-        x_woven = down_woven = None
+        x_woven, down_woven = [], []
         for a in range(PASSES):
-            parts = halves if a == last else [(0, S)]
-            picked = [held("picked_%d_%d" % (a, lo), [P, PACK, hi - lo], F32) for lo, hi in parts]
-            for i in range(PACK):
-                for part, (lo, hi) in zip(picked, parts):
-                    gather(a, i, part, lo, hi)
-                if a > 0 and i == 1:
-                    x_codes.append(held("x_%d_%d" % (a, i), [P, S], U32))
-                    quantise(x_codes[a - 1][:], x_scales[a - 1][:], x_woven[:])
-                if a > 0 and i == PACK - a:
-                    d_codes.append(held("x_%d_%d" % (a, i), [P, R], U32))
-                    quantise(d_codes[a - 1][:], d_scales[a - 1][:], down_woven[:])
+            picked = held("picked%d" % a, [P, PACK, S], F32)
+            for n in range(a * PACK, (a + 1) * PACK):
+                for lo, hi in HALVES if n == PASSES * PACK - 1 else ((0, S),):
+                    gather(n, picked, lo, hi)
+                if a > 0 and n == a * PACK + 1:
+                    x_codes.append(held("plane%d" % n, [P, S], U32))
+                    quantise(x_codes[a - 1][:], x_scales[a - 1][:], x_woven[a - 1][:])
+                if a > 0 and n == DOWN_BEFORE[a - 1] + 1:
+                    down_codes.append(held("plane%d" % n, [P, R], U32))
+                    quantise(down_codes[a - 1][:], down_scales[a - 1][:], down_woven[a - 1][:])
                     for t in range(PACK):
-                        for q in range(4):
+                        for q in range(S // QUARTER):
                             h_pass(a - 1, q, t)
-            if a < last:
-                x_woven = weave("x_woven%d" % a, picked[0][:], S, scalar_copy)
-            down_woven = weave_down(a)
+            if a < LAST:
+                x_woven.append(weave("x_woven%d" % a, picked[:], S, scalar_copy))
+            down_woven.append(weave_down(a))
+
         x_codes.append(held("x_codes_last", [P, S], U32))
-        d_codes.append(held("d_codes_last", [P, R], U32))
-        x_woven = [
-            weave("x_woven_last%d" % n, part[:], HALF, copy)
-            for n, (part, copy) in enumerate(zip(picked, (vector_copy, scalar_copy)))
+        down_codes.append(held("down_codes_last", [P, R], U32))
+        last_woven = [
+            weave("last_woven%d" % lo, picked[:, :, lo:hi], HALF, copy)
+            for (lo, hi), copy in zip(HALVES, (vector_copy, scalar_copy))
         ]
-        quantise(d_codes[last][:], d_scales[last][:], down_woven[:])
-        for half, (lo, hi) in enumerate(halves):
-            quantise(x_codes[last][:, lo:hi], x_scales[last][:, lo:hi], x_woven[half][:])
+        quantise(down_codes[LAST][:], down_scales[LAST][:], down_woven[LAST][:])
+        for half, (lo, hi) in enumerate(HALVES):
+            quantise(x_codes[LAST][:, lo:hi], x_scales[LAST][:, lo:hi], last_woven[half][:])
             if half == 0:
-                make_up(0, scalar_copy)
-            for q in (2 * half, 2 * half + 1):
+                make_up(0)
+            for q in range(lo // QUARTER, hi // QUARTER):
                 for t in range(PACK):
-                    h_pass(last, q, t)
+                    h_pass(LAST, q, t)
             bank = w4_passes(0, lo, hi)
-            make_h(half, [vector_copy, scalar_copy])
+            make_h(half)
             finish(0, lo, hi, bank)
         store(0)
+
         for c in range(1, TILES):
             if c * P % UP_CHUNK == 0:
-                make_up(c * P // UP_CHUNK, scalar_copy)
+                make_up(c * P // UP_CHUNK)
             finish(c, 0, S, w4_passes(c, 0, S))
             store(c)

from contextlib import ExitStack

import concourse.mybir as mybir
from concourse.masks import make_identity

K, M, T, S, R = 1536, 1024, 1024, 512, 512
FLOPS = 2 * S * (K * R + K * M + R * M)

F32 = mybir.dt.float32
BF16 = mybir.dt.bfloat16
I32 = mybir.dt.int32
U32 = mybir.dt.uint32
U16 = mybir.dt.uint16
U8 = mybir.dt.uint8
FP8X4 = mybir.dt.float8_e4m3fn_x4
FP4X4 = mybir.dt.float4_e2m1fn_x4
MULT = mybir.AluOpType.mult
IDENTITY = mybir.ActivationFunctionType.Identity

P = 128
PACK = 4
PASSES = K // (P * PACK)
LAST = PASSES - 1
GROUP = 16
LINE = 4
QUADRANTS = 4
HALF = S // 2
QUARTER = S // PACK
HALVES = ((0, HALF), (HALF, S))
TILES = M // P
UP_CHUNK = 2 * P
CHUNKS = M // UP_CHUNK
EARLY_COLS = UP_CHUNK
PAGES = 3
Y_BANKS = 2
Y_TILES = 4
DOWN_BEFORE = (6, 9, PASSES * PACK - 1)


def tile_list_hboth_l_bias_kernel(tc, xT, w4_words, w4_scales, down, up, wgt, b, wgo, offs, offs2, out):
    nc = tc.nc
    scalar_copy, vector_copy = nc.scalar.copy, nc.vector.tensor_copy
    with ExitStack() as ctx:
        keep = ctx.enter_context(tc.tile_pool(name="keep", bufs=1))
        y_pool = ctx.enter_context(tc.tile_pool(name="y_pool", bufs=Y_TILES))
        h_psum = ctx.enter_context(tc.psum_pool(name="h_psum", bufs=1))
        y_psum = ctx.enter_context(tc.psum_pool(name="y_psum", bufs=Y_BANKS))

        def held(name, shape, dtype):
            return keep.tile(shape, dtype, name=name, align_bytes=64)

        picks = keep.tile([P, S // GROUP], U16, name="picks")
        places = keep.tile([P, S // GROUP], U16, name="places")
        wgt_sb = held("wgt_sb", [P, S], F32)
        wgo_sb = held("wgo_sb", [P, S], F32)
        x_planes = [held("plane%d" % n, [P, T], F32) for n in range(PASSES * PACK)]
        down_raw = [held("down_raw%d" % a, [P, PACK, R], F32) for a in range(PASSES)]
        up_raw = [held("up_raw%d" % u, [P, PACK, UP_CHUNK], F32) for u in range(CHUNKS)]
        w4_early = held("w4_early", [P, PASSES, 2 * EARLY_COLS], U8)
        w4_late = held("w4_late", [P, PASSES, 2 * (M - EARLY_COLS)], U8)
        w4_scales_early = held("w4_scales_early", [P, PASSES, EARLY_COLS], U8)
        w4_scales_late = held("w4_scales_late", [P, PASSES, M - EARLY_COLS], U8)
        b_rows = held("b_rows", [P, P], F32)
        ident = held("ident", [P, P], F32)
        b_cols = held("b_cols", [P, TILES], F32)
        pages = [held("page%d" % n, [P, T], F32) for n in range(PAGES)]

        x_rows = xT.rearrange("(a p i) t -> a i p t", p=P, i=PACK)
        down_rows = down.rearrange("(a p i) r -> a p i r", p=P, i=PACK)
        up_rows = up.rearrange("(p i) n -> p i n", i=PACK)
        w4_rows = w4_words.rearrange("a p n -> p a n")

        def load_scales(queue, scales, cols):
            for quad in range(QUADRANTS):
                queue.dma_start(
                    out=scales[32 * quad : 32 * quad + 4, :, :].bitcast(I32),
                    in_=w4_scales[:, 4 * quad : 4 * quad + 4, cols].rearrange("a r n -> r a n").bitcast(I32),
                )

        def load_plane(n):
            nc.sync.dma_start(out=x_planes[n][:], in_=x_rows[n // PACK, n % PACK])

        def load_up(u):
            nc.sync.dma_start(out=up_raw[u][:], in_=up_rows[:, :, u * UP_CHUNK : (u + 1) * UP_CHUNK])

        nc.gpsimd.memset(b_rows[:], 0.0)
        make_identity(nc, ident[:])
        nc.scalar.dma_start(out=b_rows[0:TILES, :], in_=b.rearrange("(c p) -> c p", p=P))
        for scales in (w4_scales_early, w4_scales_late):
            nc.vector.memset(scales[:].rearrange("p a n -> p (a n)").bitcast(I32), 0)
        load_scales(nc.scalar, w4_scales_early, slice(0, EARLY_COLS))
        for page in pages:
            nc.vector.memset(page[:], 0.0)

        nc.sync.dma_start(picks[:], offs)
        load_plane(0)
        nc.sync.dma_start(out=wgt_sb[:], in_=wgt)
        for n in range(1, PASSES * PACK):
            if n in DOWN_BEFORE:
                a = DOWN_BEFORE.index(n)
                nc.sync.dma_start(out=down_raw[a][:], in_=down_rows[a])
            load_plane(n)
        nc.sync.dma_start(out=w4_early[:].bitcast(I32), in_=w4_rows[:, :, 0 : 2 * EARLY_COLS].bitcast(I32))
        load_up(0)
        nc.sync.dma_start(out=wgo_sb[:], in_=wgo)
        nc.sync.dma_start(places[:], offs2)
        load_scales(nc.sync, w4_scales_late, slice(EARLY_COLS, M))
        nc.sync.dma_start(out=w4_late[:].bitcast(I32), in_=w4_rows[:, :, 2 * EARLY_COLS :].bitcast(I32))
        for u in range(1, CHUNKS):
            load_up(u)

        b_bank = y_psum.tile([P, P], F32, name="y_bank")
        nc.tensor.transpose(b_bank[:], b_rows[:], ident[:])
        nc.scalar.activation(b_cols[:], b_bank[:, 0:TILES], IDENTITY)

        x_codes, down_codes = [], []
        x_scales = [held("x_scales%d" % a, [P, S], U8) for a in range(PASSES)]
        down_scales = [held("down_scales%d" % a, [P, R], U8) for a in range(PASSES)]
        up_codes = [held("up_codes%d" % u, [P, UP_CHUNK], U32) for u in range(CHUNKS)]
        up_scales = [held("up_scales%d" % u, [P, UP_CHUNK], U8) for u in range(CHUNKS)]
        h_codes = held("h_codes", [P, S], U32)
        h_scales = held("h_scales", [P, S], U8)
        h_banks = [h_psum.tile([P, PACK, QUARTER], F32, name="h_bank%d" % q) for q in range(S // QUARTER)]

        def gather(n, picked, lo, hi):
            nc.vector.tensor_tensor(
                picked[:, n % PACK, lo:hi],
                x_planes[n][:].indirect(picks[:, lo // GROUP : hi // GROUP]),
                wgt_sb[:, lo:hi],
                MULT,
            )

        def weave(name, raw, width, copy):
            woven = held(name, [P, PACK * width], BF16)
            copy(
                out=woven[:].rearrange("p (c n i) -> p c i n", n=LINE, i=PACK),
                in_=raw.rearrange("p i (c n) -> p c i n", n=LINE),
            )
            return woven

        def weave_down(a):
            woven = held("down_woven%d" % a, [P, PACK * R], BF16)
            scalar_copy(
                out=woven[:].rearrange("p (t m i) -> p m i t", t=PACK, i=PACK),
                in_=down_raw[a][:].rearrange("p i (m t) -> p m i t", t=PACK),
            )
            return woven

        def quantise(codes, scales, woven):
            nc.vector.quantize_mx(out=codes.bitcast(FP8X4), scales=scales, in_=woven)

        def make_up(u):
            woven = weave("late_woven" if u else "up_woven", up_raw[u][:], UP_CHUNK, scalar_copy)
            quantise(up_codes[u][:], up_scales[u][:], woven[:])

        def h_pass(a, q, t):
            rows, cols = slice(t * P, (t + 1) * P), slice(q * QUARTER, (q + 1) * QUARTER)
            nc.tensor.matmul_mx(
                out=h_banks[q][:, t, :],
                lhsT=down_codes[a][:, rows].bitcast(FP8X4),
                lhsT_scale=down_scales[a][:, rows],
                rhs=x_codes[a][:, cols].bitcast(FP8X4),
                rhs_scale=x_scales[a][:, cols],
                start=(a == 0 and t == 0),
                stop=(a == LAST and t == PACK - 1),
            )

        def make_h(half):
            lo, hi = HALVES[half]
            woven = held("late_woven" if half else "h_woven", [P, PACK * HALF], BF16)
            for q in range(lo // QUARTER, hi // QUARTER):
                first = PACK * (q * QUARTER - lo)
                (vector_copy if q == 0 else scalar_copy)(
                    out=woven[:, first : first + PACK * QUARTER].rearrange("p (n t) -> p n t", t=PACK),
                    in_=h_banks[q][:].rearrange("p t n -> p n t"),
                )
            quantise(h_codes[:, lo:hi], h_scales[:, lo:hi], woven[:])

        def w4_passes(c, lo, hi):
            bank = y_psum.tile([P, hi - lo], F32, name="y_bank")
            if c * P < EARLY_COLS:
                words, scales, col = w4_early, w4_scales_early, c * P
            else:
                words, scales, col = w4_late, w4_scales_late, c * P - EARLY_COLS
            width = S if hi - lo == S else QUARTER
            for a in range(PASSES):
                for j in range(lo, hi, width):
                    nc.tensor.matmul_mx(
                        out=bank[:, j - lo : j - lo + width],
                        lhsT=words[:, a, 2 * col : 2 * (col + P)].bitcast(FP4X4),
                        lhsT_scale=scales[:, a, col : col + P],
                        rhs=x_codes[a][:, j : j + width].bitcast(FP8X4),
                        rhs_scale=x_scales[a][:, j : j + width],
                        start=(a == 0 and j == lo),
                        stop=False,
                    )
            return bank

        def finish(c, lo, hi, bank):
            u, col = divmod(c * P, UP_CHUNK)
            nc.tensor.matmul_mx(
                out=bank[:],
                lhsT=up_codes[u][:, col : col + P].bitcast(FP8X4),
                lhsT_scale=up_scales[u][:, col : col + P],
                rhs=h_codes[:, lo:hi].bitcast(FP8X4),
                rhs_scale=h_scales[:, lo:hi],
                start=False,
                stop=True,
            )
            y = y_pool.tile([P, hi - lo], F32, name="y", align_bytes=64)
            nc.scalar.activation(y[:], bank[:], IDENTITY, bias=b_cols[:, c : c + 1])
            nc.vector.tensor_tensor(
                pages[c % PAGES][:].indirect(places[:, lo // GROUP : hi // GROUP]), y[:], wgo_sb[:, lo:hi], MULT
            )

        def store(c):
            nc.sync.dma_start(out=out[c * P : (c + 1) * P, :], in_=pages[c % PAGES][:])

        x_woven, down_woven = [], []
        for a in range(PASSES):
            picked = held("picked%d" % a, [P, PACK, S], F32)
            for n in range(a * PACK, (a + 1) * PACK):
                for lo, hi in HALVES if n == PASSES * PACK - 1 else ((0, S),):
                    gather(n, picked, lo, hi)
                if a > 0 and n == a * PACK + 1:
                    x_codes.append(held("plane%d" % n, [P, S], U32))
                    quantise(x_codes[a - 1][:], x_scales[a - 1][:], x_woven[a - 1][:])
                if a > 0 and n == DOWN_BEFORE[a - 1] + 1:
                    down_codes.append(held("plane%d" % n, [P, R], U32))
                    quantise(down_codes[a - 1][:], down_scales[a - 1][:], down_woven[a - 1][:])
                    for t in range(PACK):
                        for q in range(S // QUARTER):
                            h_pass(a - 1, q, t)
            if a < LAST:
                x_woven.append(weave("x_woven%d" % a, picked[:], S, scalar_copy))
            down_woven.append(weave_down(a))

        x_codes.append(held("x_codes_last", [P, S], U32))
        down_codes.append(held("down_codes_last", [P, R], U32))
        last_woven = [
            weave("last_woven%d" % lo, picked[:, :, lo:hi], HALF, copy)
            for (lo, hi), copy in zip(HALVES, (vector_copy, scalar_copy))
        ]
        quantise(down_codes[LAST][:], down_scales[LAST][:], down_woven[LAST][:])
        for half, (lo, hi) in enumerate(HALVES):
            quantise(x_codes[LAST][:, lo:hi], x_scales[LAST][:, lo:hi], last_woven[half][:])
            if half == 0:
                make_up(0)
            for q in range(lo // QUARTER, hi // QUARTER):
                for t in range(PACK):
                    h_pass(LAST, q, t)
            bank = w4_passes(0, lo, hi)
            make_h(half)
            finish(0, lo, hi, bank)
        store(0)

        for c in range(1, TILES):
            if c * P % UP_CHUNK == 0:
                make_up(c * P // UP_CHUNK)
            finish(c, 0, S, w4_passes(c, 0, S))
            store(c)
